import numpy as np
import ml_dtypes


def mxq(x, axis, fmt="e4m3"):
    dtype, down = {"e4m3": (ml_dtypes.float8_e4m3fn, 7), "e5m2": (ml_dtypes.float8_e5m2, 14)}[fmt]
    v = np.moveaxis(np.asarray(x, np.float32).astype(ml_dtypes.bfloat16).astype(np.float64), axis, -1)
    blocks = v.reshape(v.shape[:-1] + (-1, 32))
    amax = np.abs(blocks).max(-1, keepdims=True)
    byte = np.maximum(np.where(amax > 0, np.frexp(amax)[1] - 1 + 127, 0) - down, 1)
    scale = np.exp2(byte - 127.0)
    codes = (blocks / scale).astype(np.float32).astype(dtype).astype(np.float64)
    return np.moveaxis((codes * scale).reshape(v.shape), -1, axis)


WIDE = False


def mx_kscale(k):
    if not WIDE:
        return np.ones(k)
    levels = np.array([10, -10, 5, -5, 0])
    if k % 512:
        return np.exp2(np.random.permutation(np.resize(levels, k // 32))).repeat(32)
    a = np.empty((k // 512, 16))
    for p in range(k // 512):
        a[p, :8] = np.random.permutation(np.resize(levels, 8))
        for g in range(8):
            far = levels[np.abs(levels - a[p, g]) >= 10]
            a[p, g + 8] = far[np.random.randint(len(far))]
    return np.exp2(a.ravel()).repeat(32)


def f64(x):
    return np.asarray(x).astype(np.float64)


def striped(idx):
    return np.tile(idx.reshape(-1, 16).T, (8, 1)).astype(np.uint16)


def unstriped(offs):
    return offs[:16].T.reshape(-1).astype(np.int64)


def striped8(idx):
    return np.concatenate([x.reshape(-1, 16).T for x in idx]).astype(np.uint16)


def runs(offs, k):
    lists = np.stack([offs[16 * r : 16 * r + 16].T.reshape(-1) for r in range(8)]).astype(np.int64)
    return lists[np.arange(k) % 512 // 64]


def pack_weight(w):
    k, n = w.shape
    w = f64(np.asarray(w, np.float32).astype(ml_dtypes.bfloat16)).reshape(k // 32, 32, n)
    amax = np.abs(w).max(1)
    byte = np.clip(np.where(amax > 0, np.frexp(amax)[1] - 1 + 127 - 7, 1), 1, 254)
    scaled = (w * np.exp2(127.0 - byte)[:, None, :]).reshape(k, n).astype(np.float32)
    words = np.ascontiguousarray(scaled.reshape(k // 512, 128, 4, n).transpose(0, 1, 3, 2)).astype(ml_dtypes.float8_e4m3fn).view(np.uint8)
    return words, np.ascontiguousarray(byte.astype(np.uint8).reshape(k // 512, 16, n))


def unpack_weight(words, scales):
    g, p, n, _ = words.shape
    vals = np.ascontiguousarray(words).view(ml_dtypes.float8_e4m3fn).astype(np.float64) * np.repeat(np.exp2(scales.astype(np.float64) - 127.0), 8, axis=1)[..., None]
    return vals.transpose(0, 1, 3, 2).reshape(g * 512, n)


E2M1 = np.array([0.0, 0.5, 1.0, 1.5, 2.0, 3.0, 4.0, 6.0, -0.0, -0.5, -1.0, -1.5, -2.0, -3.0, -4.0, -6.0])


def pack_fp4(w):
    k, n = w.shape
    w = f64(np.asarray(w, np.float32).astype(ml_dtypes.bfloat16)).reshape(k // 32, 32, n)
    amax = np.abs(w).max(1)
    mant, ex = np.frexp(amax / 6.0)
    byte = np.clip(np.where(amax > 0, np.where(mant > 0.5, ex, ex - 1) + 127, 1), 1, 254)
    scaled = (w * np.exp2(127.0 - byte)[:, None, :]).reshape(k, n).astype(np.float32)
    c = np.ascontiguousarray(scaled.reshape(k // 512, 128, 4, n).transpose(0, 1, 3, 2)).astype(ml_dtypes.float4_e2m1fn).view(np.uint8) & 0xF
    words = (c[..., 0::2] | (c[..., 1::2] << 4)).reshape(k // 512, 128, 2 * n)
    return np.ascontiguousarray(words), np.ascontiguousarray(byte.astype(np.uint8).reshape(k // 512, 16, n))


def unpack_fp4(words, scales):
    g, _, n = scales.shape
    words = np.ascontiguousarray(words).reshape(g, 128, n, 2)
    nib = np.empty((g, 128, n, 4), np.uint8)
    nib[..., 0::2] = words & 0xF
    nib[..., 1::2] = words >> 4
    vals = E2M1[nib] * np.repeat(np.exp2(scales.astype(np.float64) - 127.0), 8, axis=1)[..., None]
    return vals.transpose(0, 1, 3, 2).reshape(g * 512, n)


def sigmoid(v):
    return 1.0 / (1.0 + np.exp(-np.maximum(v, -700.0)))

def planes(y):
    n, m = y.shape
    v = y.astype(np.float32).astype(ml_dtypes.bfloat16).astype(np.float64).reshape(n // 32, 32, m)
    top = np.abs(v).max(1)
    byte = np.clip(np.where(top > 0, np.frexp(top)[1] - 1 + 127 - 7, 1), 1, 254)
    codes = (v * np.exp2(127.0 - byte)[:, None, :]).reshape(n, m).astype(np.float32).astype(ml_dtypes.float8_e4m3fn).view(np.uint8)
    words = codes.reshape(n // 512, 128, 4, m).transpose(0, 1, 3, 2)
    return np.ascontiguousarray(words), np.ascontiguousarray(byte.astype(np.uint8).reshape(n // 512, 16, m))


K, T, S, V, H = 512, 2048, 512, 512, 512


def setup_inputs():
    n = np.random.standard_normal
    s = mx_kscale(K)[:, None]
    u = mx_kscale(S)
    packed_xT = pack_weight(n((K, T)) * s)
    packed_w1 = pack_fp4(n((K, H)) / np.sqrt(K) / s)
    packed_w2 = pack_fp4(n((K, H)) / np.sqrt(K) / s)
    packed_w3 = pack_fp4(n((K, H)) / np.sqrt(K) / s)
    return {
        "x_words": packed_xT[0],
        "x_scales": packed_xT[1],
        "w1_words": packed_w1[0],
        "w1_scales": packed_w1[1],
        "w2_words": packed_w2[0],
        "w2_scales": packed_w2[1],
        "w3_words": packed_w3[0],
        "w3_scales": packed_w3[1],
        "ga": (np.random.uniform(0.5, 1.5, (H, 1)) * u[:, None]).astype(np.float32),
        "gb": (np.random.uniform(0.5, 1.5, (H, 1)) / u[:, None]).astype(np.float32),
        "offs": striped(np.random.permutation(T)[:S]),
        "two": striped(np.random.permutation(T)[:S]),
        "n1": striped8(np.stack([np.random.permutation(S) for _ in range(8)])),
        "n2": striped8(np.stack([np.random.permutation(S) for _ in range(8)])),
        "n3": striped8(np.stack([np.random.permutation(S) for _ in range(8)])),
        "three": striped(np.random.permutation(T)[:V]),
        "n4": striped8(np.stack([np.random.permutation(V) for _ in range(8)])),
        "n5": striped8(np.stack([np.random.permutation(V) for _ in range(8)])),
        "n6": striped8(np.stack([np.random.permutation(V) for _ in range(8)])),
        "n7": striped8(np.stack([np.random.permutation(V) for _ in range(8)])),
    }


def reference(x_words, x_scales, w1_words, w1_scales, w2_words, w2_scales, w3_words, w3_scales, ga, gb, offs, two, n1, n2, n3, three, n4, n5, n6, n7):
    x_two = unpack_weight(x_words, x_scales)[:, unstriped(two)]
    d = unpack_fp4(w2_words, w2_scales).T @ x_two
    xq = unpack_weight(x_words, x_scales)[:, unstriped(offs)]
    y = unpack_fp4(w1_words, w1_scales).T @ xq
    z = f64(ga) * (d * (y[np.arange(H)[:, None], runs(n1, H)] - y) + 0.5 * ((d[np.arange(H)[:, None], runs(n3, H)]) * (y[np.arange(H)[:, None], runs(n2, H)] - y)))
    x_three = unpack_weight(x_words, x_scales)[:, unstriped(three)]
    b = unpack_fp4(w3_words, w3_scales).T @ x_three
    b1 = b[np.arange(H)[:, None], runs(n4, H)]
    b2 = b[np.arange(H)[:, None], runs(n5, H)]
    b3 = b[np.arange(H)[:, None], runs(n6, H)]
    z2 = f64(gb) * (np.maximum(np.maximum(b1, b2), b3) - (0.5 * (np.maximum(np.minimum(b1, b2), np.minimum(np.maximum(b1, b2), b3)))))
    s = 0.0625 * ((mxq(z, 0, "e4m3").T @ mxq(z2, 0, "e4m3")))
    st = s * (sigmoid(s[np.arange(S)[:, None], runs(n7, S)]))
    out_0 = np.maximum(st, st[np.arange(S)[:, None], runs(n7, S)])
    return (out_0,) + planes(out_0)

@@ -1,0 +1,355 @@
+from contextlib import ExitStack
+
+import concourse.mybir as mybir
+from concourse.masks import make_identity
+
+K, T, S, V, H = 512, 2048, 512, 512, 512
+FLOPS = 4 * 2 * 512 * 512 * 512
+
+F32 = mybir.dt.float32
+BF16 = mybir.dt.bfloat16
+I32 = mybir.dt.int32
+U32 = mybir.dt.uint32
+U16 = mybir.dt.uint16
+U8 = mybir.dt.uint8
+FP8X4 = mybir.dt.float8_e4m3fn_x4
+FP4X4 = mybir.dt.float4_e2m1fn_x4
+ALU = mybir.AluOpType
+ACT = mybir.ActivationFunctionType
+
+P = 128
+SLOTS = 4
+HALF = 256
+Z2_PIECES = ((0, 256), (256, 128), (384, 128))
+AFTER = {("b1", 1): "gap120", ("gap12", 1): "gap30", ("b1", 2): "gap121", ("gap12", 2): "z2_bf0", ("lift", 1): "rounded_held", ("lift", 2): "z2_bf1"}
+
+
+def tile_picked_twkflowbtop2twicp_none_po_kernel(
+    tc, x_words, x_scales, w1_words, w1_scales, w2_words, w2_scales, w3_words, w3_scales,
+    ga, gb, offs, two, n1, n2, n3, three, n4, n5, n6, n7, out_0, out_1, out_2,
+):
+    nc = tc.nc
+    with ExitStack() as ctx:
+        keep = ctx.enter_context(tc.tile_pool(name="keep", bufs=1))
+        ring = ctx.enter_context(tc.tile_pool(name="ring", bufs=2))
+        psum = ctx.enter_context(tc.psum_pool(name="psum", bufs=2))
+
+        def new(name, shape, dtype, tag=None):
+            return keep.tile(shape, dtype, name=name, tag=tag or name, align_bytes=64)
+
+        def load_list(name, src):
+            lst = new(name, [P, 32], U16)
+            nc.sync.dma_start(lst[:], src)
+            return lst
+
+        def entries(lst, c0, n):
+            return lst[:, c0 // 16 : (c0 + n) // 16]
+
+        def load_scale_rows(plane, src):
+            rows = src[0].bitcast(I32)
+            for q in range(4):
+                nc.sync.dma_start(plane[32 * q : 32 * q + 4, :].bitcast(I32), rows[4 * q : 4 * q + 4, :])
+
+        xs = new("xs", [P, T], U8)
+        nc.gpsimd.memset(xs[:].bitcast(I32), 0)
+        ws_raw = [new("ws_raw%d" % i, [P, H], U8) for i in range(3)]
+        for plane in ws_raw:
+            nc.vector.memset(plane[:].bitcast(I32), 0)
+        gain_rows = new("gain_rows", [P, H], F32)
+        nc.gpsimd.memset(gain_rows[:], 0.0)
+        ident = new("ident", [P, P], F32)
+        make_identity(nc, ident[:])
+
+        warm = new("warm", [P, 1], F32)
+        nc.scalar.activation(warm[:], ident[:, 0:1], ACT.Sigmoid)
+        xw = new("xw", [P, T], I32)
+        nc.sync.dma_start(xw[:], x_words[0].rearrange("p n t -> p (n t)").bitcast(I32))
+        ww_raw = [new("ww_raw%d" % i, [P, H // 2], I32) for i in range(3)]
+        load_scale_rows(xs, x_scales)
+        l_offs = load_list("l_offs", offs)
+        l_two = load_list("l_two", two)
+        l_three = load_list("l_three", three)
+
+        nc.sync.dma_start(ww_raw[0][:], w1_words[0].bitcast(I32))
+        load_scale_rows(ws_raw[0], w1_scales)
+        l1 = load_list("l1", n1)
+        l2 = load_list("l2", n2)
+        nc.sync.dma_start(ww_raw[1][:], w2_words[0].bitcast(I32))
+        load_scale_rows(ws_raw[1], w2_scales)
+        for row, gain in enumerate((ga, gb)):
+            nc.sync.dma_start(
+                gain_rows[row : row + 1, :].rearrange("o (t b c) -> o t b c", t=SLOTS, c=8),
+                gain.rearrange("(b t c) o -> o t b c", t=SLOTS, c=8),
+            )
+        l3 = load_list("l3", n3)
+        nc.sync.dma_start(ww_raw[2][:], w3_words[0].bitcast(I32))
+        load_scale_rows(ws_raw[2], w3_scales)
+        l4 = load_list("l4", n4)
+        l5 = load_list("l5", n5)
+        l6 = load_list("l6", n6)
+        l7 = load_list("l7", n7)
+
+        def pick_scales(name, lst, tag=None):
+            picked = new(name, [P, S], U8, tag)
+            nc.vector.tensor_copy(picked[:], xs[:].indirect(lst[:]))
+            return picked
+
+        def pick_words(name, lst, tag=None):
+            picked = new(name, [P, S], U32, tag)
+            nc.vector.tensor_copy(picked[:], xw[:].bitcast(U32).indirect(lst[:]))
+            return picked
+
+        def deal_weight(i):
+            words = new("ww%d" % i, [P, 2 * H], U8)
+            scales = new("ws%d" % i, [P, H], U8)
+            nc.vector.tensor_copy(
+                words[:].bitcast(I32).rearrange("p (t b w) -> p t b w", t=SLOTS, w=4),
+                ww_raw[i][:].rearrange("p (b t w) -> p t b w", t=SLOTS, w=4),
+            )
+            nc.vector.tensor_copy(
+                scales[:].bitcast(I32).rearrange("p (t b w) -> p t b w", t=SLOTS, w=2),
+                ws_raw[i][:].bitcast(I32).rearrange("p (b t w) -> p t b w", t=SLOTS, w=2),
+            )
+            return words, scales
+
+        def project(weight, picked, t):
+            bank = psum.tile([P, S], F32, name="product", tag="product", bufs=4)
+            nc.tensor.matmul_mx(
+                bank[:],
+                lhsT=weight[0][:, 2 * P * t : 2 * P * (t + 1)].bitcast(FP4X4),
+                lhsT_scale=weight[1][:, P * t : P * (t + 1)],
+                rhs=picked[0][:].bitcast(FP8X4),
+                rhs_scale=picked[1][:],
+                start=True,
+                stop=True,
+            )
+            return bank
+
+        x_offs = (pick_words("x_offs", l_offs), pick_scales("s_offs", l_offs))
+        w1 = deal_weight(0)
+        x_two = (pick_words("x_two", l_two, "ws_raw0"), pick_scales("s_two", l_two))
+        w2 = deal_weight(1)
+
+        gain_bank = psum.tile([P, SLOTS, P], F32, name="summed", tag="summed")
+        for t in range(SLOTS):
+            nc.tensor.transpose(gain_bank[:, t, :], gain_rows[:, P * t : P * (t + 1)], ident[:])
+        half_sign = new("half_sign", [P, SLOTS, 1], F32)
+        nc.vector.tensor_scalar(half_sign[:], gain_bank[:, :, 1:2], 0.0, 0.5, ALU.is_ge, ALU.subtract)
+        gains = new("gains", [P, SLOTS, 2], F32)
+        nc.vector.tensor_tensor(gains[:], gain_bank[:, :, 0:2], half_sign[:].to_broadcast([P, SLOTS, 2]), ALU.mult)
+
+        x_three = (pick_words("x_three", l_three, "ws_raw1"), pick_scales("s_three", l_three, "ww_raw1"))
+        w3 = deal_weight(2)
+
+        y_win = [new("y_win%d" % t, [P, 2 * S], F32) for t in range(SLOTS)]
+        d_win = [new("d_win%d" % t, [P, 2 * S], F32) for t in range(SLOTS)]
+        b_win = [new("b_win%d" % t, [P, V], F32) for t in range(SLOTS)]
+        for pair in range(2):
+            for t in (2 * pair, 2 * pair + 1):
+                bank = project(w1, x_offs, t)
+                nc.scalar.copy(y_win[t][:, 0:S], bank[:])
+                nc.scalar.copy(y_win[t ^ 1][:, S : 2 * S], bank[:])
+            for t in (2 * pair, 2 * pair + 1):
+                bank = project(w2, x_two, t)
+                nc.scalar.activation(d_win[t][:, 0:S], bank[:], ACT.Copy, scale=gains[:, t, 0:1])
+        for t in range(SLOTS):
+            bank = project(w3, x_three, t)
+            nc.scalar.activation(b_win[t][:], bank[:], ACT.Copy, scale=gains[:, t, 1:2])
+
+        pull2 = new("pull2", [P, SLOTS, S], F32)
+        term1 = new("term1", [P, SLOTS, S], F32)
+        term2 = new("term2", [P, SLOTS, S], F32)
+
+        def z_pulls(t):
+            y_plain = y_win[t ^ 1][:, S : 2 * S]
+            nc.vector.tensor_tensor(d_win[t][:, S : 2 * S], y_win[t][:].indirect(l1[:]), y_plain, ALU.subtract)
+            nc.vector.tensor_tensor(pull2[:, t, :], y_win[t][:].indirect(l2[:]), y_plain, ALU.subtract)
+
+        def z_terms(t):
+            nc.vector.scalar_tensor_tensor(term1[:, t, :], d_win[t][:, 0:S], 2.0, d_win[t][:, S : 2 * S], ALU.mult, ALU.mult)
+            nc.vector.tensor_tensor(term2[:, t, :], d_win[t][:].indirect(l3[:]), pull2[:, t, :], ALU.mult)
+
+        z_pulls(0)
+        for t in range(1, SLOTS):
+            z_pulls(t)
+            z_terms(t - 1)
+        z_terms(SLOTS - 1)
+
+        def sum_round_turn(terms, c0, held=False):
+            summed = psum.tile([P, SLOTS, P], F32, name="summed", tag="summed")
+            for t in range(SLOTS):
+                for i, term in enumerate(terms):
+                    nc.tensor.matmul(
+                        summed[:, t, :], term[:, t, c0 : c0 + P], ident[:],
+                        start=(i == 0), stop=(i == len(terms) - 1), is_transpose=True,
+                    )
+            rounded = new("rounded_held", [P, SLOTS * P], BF16) if held else ring.tile([P, SLOTS * P], BF16, name="rounded")
+            nc.scalar.copy(
+                rounded[:].rearrange("j (u p e) -> j u p e", u=2, e=2),
+                summed[:].rearrange("j (u e) p -> j u p e", e=2),
+            )
+            turned = psum.tile([P, 2, P], F32, name="turned", tag="turned")
+            for u in range(2):
+                nc.tensor.transpose(turned[:, u, :], rounded[:].bitcast(F32)[:, P * u : P * (u + 1)], ident[:])
+            return turned
+
+        z_bf = new("z_bf", [P, SLOTS * S], BF16)
+        z_pairs = z_bf[:].bitcast(F32).rearrange("p (t m u) -> p t m u", t=SLOTS, u=2)
+        for blk in range(S // P):
+            turned = sum_round_turn((term1, term2), P * blk)
+            nc.scalar.copy(z_pairs[:, :, 32 * blk : 32 * (blk + 1), :], turned[:].rearrange("p u (m t) -> p t m u", t=SLOTS))
+        z_codes = new("z_codes", [P, S], U32)
+        z_scales = new("z_scales", [P, S], U8)
+
+        z2_codes = new("z2_codes", [P, V], U32)
+        z2_scales = new("z2_scales", [P, V], U8)
+        s_bank = [psum.tile([P, V], F32, name="product", tag="product", bufs=4) for t in range(SLOTS)]
+        s_win = [new("s_win%d" % t, [P, V], F32) for t in range(SLOTS)]
+        work = {}
+
+        def flat(tile):
+            return tile[:].rearrange("p t c -> p (t c)")
+
+        def z2_first(i):
+            c0, n = Z2_PIECES[i]
+            w = {name: new("%s%d" % (name, i), [P, SLOTS, n], F32, AFTER.get((name, i))) for name in ("b1", "gap12", "span", "top12", "gap3", "low")}
+            work[i] = w
+            for t in range(SLOTS):
+                nc.vector.tensor_copy(w["b1"][:, t, :], b_win[t][:].indirect(entries(l4, c0, n)))
+            for t in range(SLOTS):
+                nc.vector.tensor_tensor(w["gap12"][:, t, :], b_win[t][:].indirect(entries(l5, c0, n)), w["b1"][:, t, :], ALU.subtract)
+            nc.scalar.activation(flat(w["span"]), flat(w["gap12"]), ACT.Abs)
+
+        def z2_top(i):
+            w = work[i]
+            nc.vector.scalar_tensor_tensor(flat(w["top12"]), flat(w["gap12"]), 0.0, flat(w["b1"]), ALU.max, ALU.add)
+
+        def z2_third(i):
+            c0, n = Z2_PIECES[i]
+            w = work[i]
+            for t in range(SLOTS):
+                nc.vector.tensor_tensor(w["gap3"][:, t, :], b_win[t][:].indirect(entries(l6, c0, n)), w["top12"][:, t, :], ALU.subtract)
+
+        def z2_low(i):
+            w = work[i]
+            nc.vector.scalar_tensor_tensor(flat(w["low"]), flat(w["gap3"]), -1.0, flat(w["span"]), ALU.mult, ALU.min)
+
+        def z2_sum(i):
+            c0, n = Z2_PIECES[i]
+            w = work[i]
+            w["lift"] = new("lift%d" % i, [P, SLOTS, n], F32, AFTER.get(("lift", i)))
+            w["bf"] = new("z2_bf%d" % i, [P, SLOTS * n], BF16)
+            if i < len(Z2_PIECES) - 1:
+                nc.scalar.activation(flat(w["lift"]), flat(w["low"]), ACT.Relu, scale=-3.0)
+                pairs = w["bf"][:].bitcast(F32).rearrange("p (v u) -> p v u", u=2)
+                for blk in range(n // P):
+                    turned = sum_round_turn((w["top12"], w["low"], w["lift"]), P * blk, (i, blk) == (0, 1))
+                    nc.scalar.copy(pairs[:, P * blk : P * (blk + 1), :], turned[:].rearrange("p u v -> p v u"))
+            else:
+                nc.vector.scalar_tensor_tensor(flat(w["lift"]), flat(w["low"]), -2.0, flat(w["low"]), ALU.mult, ALU.max)
+                nc.vector.tensor_tensor(
+                    w["bf"][:].rearrange("p (c i t) -> p c t i", i=2, t=SLOTS),
+                    w["lift"][:].rearrange("p t (c i) -> p c t i", i=2),
+                    w["top12"][:].rearrange("p t (c i) -> p c t i", i=2),
+                    ALU.add,
+                )
+
+        def z2_quantise(i):
+            c0, n = Z2_PIECES[i]
+            cols = slice(c0, c0 + n)
+            nc.vector.quantize_mx(z2_codes[:, cols].bitcast(FP8X4), z2_scales[:, cols], work[i]["bf"][:])
+
+        def scores(i, t):
+            c0, n = Z2_PIECES[i]
+            cols = slice(c0, c0 + n)
+            nc.tensor.matmul_mx(
+                s_bank[t][:, cols],
+                lhsT=z_codes[:, P * t : P * (t + 1)].bitcast(FP8X4),
+                lhsT_scale=z_scales[:, P * t : P * (t + 1)],
+                rhs=z2_codes[:, cols].bitcast(FP8X4),
+                rhs_scale=z2_scales[:, cols],
+                start=True,
+                stop=True,
+            )
+            nc.scalar.activation(s_win[t][:, cols], s_bank[t][:, cols], ACT.Copy, scale=0.0625)
+
+        z2_first(0)
+        z2_top(0)
+        z2_third(0)
+        z2_low(0)
+        z2_sum(0)
+        nc.vector.quantize_mx(z_codes[:].bitcast(FP8X4), z_scales[:], z_bf[:])
+        z2_first(1)
+        z2_top(1)
+        z2_third(1)
+        z2_low(1)
+        z2_quantise(0)
+        z2_sum(1)
+        for t in range(SLOTS):
+            scores(0, t)
+        z2_first(2)
+        z2_top(2)
+        z2_third(2)
+        z2_low(2)
+        z2_quantise(1)
+        for t in range(SLOTS):
+            scores(1, t)
+        z2_sum(2)
+        z2_quantise(2)
+
+        out_rows = out_0.rearrange("(p t) c -> p t c", t=SLOTS)
+        gate = new("gate", [P, SLOTS, V], F32)
+        st_win = [new("st_win%d" % t, [P, V], F32) for t in range(SLOTS)]
+        other = [new("other%d" % h, [P, SLOTS, HALF], F32) for h in range(2)]
+        res = [new("res%d" % h, [P, SLOTS, HALF], F32) for h in range(2)]
+        res_bf = [new("res_bf%d" % h, [P, SLOTS * HALF], BF16) for h in range(2)]
+        res_codes = new("res_codes", [P, V], U32)
+        res_scales = new("res_scales", [P, V], U8)
+        out_words = out_1[0].rearrange("p c t -> p (c t)").bitcast(I32)
+
+        def gated(t):
+            scores(len(Z2_PIECES) - 1, t)
+            for h in range(2):
+                nc.scalar.activation(gate[:, t, HALF * h : HALF * (h + 1)], s_win[t][:].indirect(entries(l7, HALF * h, HALF)), ACT.Sigmoid)
+            nc.vector.tensor_tensor(st_win[t][:], s_win[t][:], gate[:, t, :], ALU.mult)
+
+        def fetch(t, h):
+            nc.vector.tensor_copy(other[h][:, t, :], st_win[t][:].indirect(entries(l7, HALF * h, HALF)))
+
+        def larger(t, h):
+            cols = slice(HALF * h, HALF * (h + 1))
+            nc.vector.tensor_tensor(res[h][:, t, :], st_win[t][:, cols], other[h][:, t, :], ALU.max)
+            nc.sync.dma_start(out_rows[:, t, cols], res[h][:, t, :])
+
+        def weave(engine_copy, h, c0, c1):
+            engine_copy(
+                res_bf[h][:, SLOTS * c0 : SLOTS * c1].rearrange("p (c i t) -> p c t i", i=4, t=SLOTS),
+                res[h][:, :, c0:c1].rearrange("p t (c i) -> p c t i", i=4),
+            )
+
+        def hand_on(h):
+            cols = slice(HALF * h, HALF * (h + 1))
+            nc.vector.quantize_mx(res_codes[:, cols].bitcast(FP8X4), res_scales[:, cols], res_bf[h][:])
+            nc.scalar.dma_start(out_words[:, cols], res_codes[:, cols].bitcast(I32))
+
+        gated(0)
+        fetch(0, 0)
+        for t in range(1, SLOTS):
+            gated(t)
+            larger(t - 1, 0)
+            fetch(t, 0)
+        fetch(0, 1)
+        larger(SLOTS - 1, 0)
+        weave(nc.scalar.copy, 0, 0, HALF)
+        for t in range(1, SLOTS):
+            fetch(t, 1)
+            larger(t - 1, 1)
+        hand_on(0)
+        larger(SLOTS - 1, 1)
+        weave(nc.vector.tensor_copy, 1, 0, 160)
+        weave(nc.scalar.copy, 1, 160, HALF)
+        hand_on(1)
+        scale_rows = out_2[0].bitcast(I32)
+        for q in range(4):
+            queue = nc.sync if q % 2 == 0 else nc.scalar
+            queue.dma_start(scale_rows[4 * q : 4 * q + 4, :], res_scales[32 * q : 32 * q + 4, :].bitcast(I32))

@@ -20,8 +20,9 @@ ACT = mybir.ActivationFunctionType
 P = 128
 SLOTS = 4
 HALF = 256
-Z2_PIECES = ((0, 256), (256, 128), (384, 128))
-AFTER = {("b1", 1): "gap120", ("gap12", 1): "gap30", ("b1", 2): "gap121", ("gap12", 2): "z2_bf0", ("lift", 1): "rounded_held", ("lift", 2): "z2_bf1"}
+X_FIRST = 512
+Z2_PIECES = ((0, 256), (256, 256))
+AFTER = {("lift", 0): "pull2", ("gap12", 1): "z_bf", ("low", 1): "z2_bf0"}
 
 
 def tile_picked_twkflowbtop2twicp_none_po_kernel(
@@ -63,10 +64,12 @@ def tile_picked_twkflowbtop2twicp_none_po_kernel(
         warm = new("warm", [P, 1], F32)
         nc.scalar.activation(warm[:], ident[:, 0:1], ACT.Sigmoid)
         xw = new("xw", [P, T], I32)
-        nc.sync.dma_start(xw[:], x_words[0].rearrange("p n t -> p (n t)").bitcast(I32))
+        x_rows = x_words[0].rearrange("p n t -> p (n t)").bitcast(I32)
+        nc.sync.dma_start(xw[:, 0:X_FIRST], x_rows[:, 0:X_FIRST])
         ww_raw = [new("ww_raw%d" % i, [P, H // 2], I32) for i in range(3)]
         load_scale_rows(xs, x_scales)
         l_offs = load_list("l_offs", offs)
+        nc.sync.dma_start(xw[:, X_FIRST:T], x_rows[:, X_FIRST:T])
         l_two = load_list("l_two", two)
         l_three = load_list("l_three", three)
 
@@ -125,7 +128,8 @@ def tile_picked_twkflowbtop2twicp_none_po_kernel(
             )
             return bank
 
-        x_offs = (pick_words("x_offs", l_offs), pick_scales("s_offs", l_offs))
+        s_offs = pick_scales("s_offs", l_offs)
+        x_offs = (pick_words("x_offs", l_offs), s_offs)
         w1 = deal_weight(0)
         x_two = (pick_words("x_two", l_two, "ws_raw0"), pick_scales("s_two", l_two))
         w2 = deal_weight(1)
@@ -143,7 +147,7 @@ def tile_picked_twkflowbtop2twicp_none_po_kernel(
 
         y_win = [new("y_win%d" % t, [P, 2 * S], F32) for t in range(SLOTS)]
         d_win = [new("d_win%d" % t, [P, 2 * S], F32) for t in range(SLOTS)]
-        b_win = [new("b_win%d" % t, [P, V], F32) for t in range(SLOTS)]
+        b_win = [new("b_win%d" % t, [P, 2 * V], F32) for t in range(SLOTS)]
         for pair in range(2):
             for t in (2 * pair, 2 * pair + 1):
                 bank = project(w1, x_offs, t)
@@ -154,10 +158,12 @@ def tile_picked_twkflowbtop2twicp_none_po_kernel(
                 nc.scalar.activation(d_win[t][:, 0:S], bank[:], ACT.Copy, scale=gains[:, t, 0:1])
         for t in range(SLOTS):
             bank = project(w3, x_three, t)
-            nc.scalar.activation(b_win[t][:], bank[:], ACT.Copy, scale=gains[:, t, 1:2])
+            nc.scalar.activation(b_win[t][:, 0:V], bank[:], ACT.Copy, scale=gains[:, t, 1:2])
+
+        for t in range(SLOTS):
+            nc.scalar.activation(b_win[t][:, V : 2 * V], d_win[t][:, 0:S], ACT.Copy, scale=2.0)
 
         pull2 = new("pull2", [P, SLOTS, S], F32)
-        term1 = new("term1", [P, SLOTS, S], F32)
         term2 = new("term2", [P, SLOTS, S], F32)
 
         def z_pulls(t):
@@ -165,17 +171,24 @@ def tile_picked_twkflowbtop2twicp_none_po_kernel(
             nc.vector.tensor_tensor(d_win[t][:, S : 2 * S], y_win[t][:].indirect(l1[:]), y_plain, ALU.subtract)
             nc.vector.tensor_tensor(pull2[:, t, :], y_win[t][:].indirect(l2[:]), y_plain, ALU.subtract)
 
-        def z_terms(t):
-            nc.vector.scalar_tensor_tensor(term1[:, t, :], d_win[t][:, 0:S], 2.0, d_win[t][:, S : 2 * S], ALU.mult, ALU.mult)
+        def z_term2(t):
             nc.vector.tensor_tensor(term2[:, t, :], d_win[t][:].indirect(l3[:]), pull2[:, t, :], ALU.mult)
 
         z_pulls(0)
         for t in range(1, SLOTS):
             z_pulls(t)
-            z_terms(t - 1)
-        z_terms(SLOTS - 1)
+            z_term2(t - 1)
+        z_term2(SLOTS - 1)
+        term1 = new("term1", [P, SLOTS, S], F32, "pull2")
+        b1 = new("b1", [P, SLOTS, V], F32, "y_win3")
+        for h in range(2):
+            cols = slice(HALF * h, HALF * (h + 1))
+            for t in range(SLOTS):
+                nc.gpsimd.tensor_tensor(term1[:, t, cols], b_win[t][:, V + HALF * h : V + HALF * (h + 1)], d_win[t][:, S + HALF * h : S + HALF * (h + 1)], ALU.mult)
+        for t in range(SLOTS):
+            nc.vector.tensor_copy(b1[:, t, :], b_win[t][:].indirect(l4[:]))
 
-        def sum_round_turn(terms, c0, held=False):
+        def sum_round_turn(terms, c0):
             summed = psum.tile([P, SLOTS, P], F32, name="summed", tag="summed")
             for t in range(SLOTS):
                 for i, term in enumerate(terms):
@@ -183,7 +196,7 @@ def tile_picked_twkflowbtop2twicp_none_po_kernel(
                         summed[:, t, :], term[:, t, c0 : c0 + P], ident[:],
                         start=(i == 0), stop=(i == len(terms) - 1), is_transpose=True,
                     )
-            rounded = new("rounded_held", [P, SLOTS * P], BF16) if held else ring.tile([P, SLOTS * P], BF16, name="rounded")
+            rounded = ring.tile([P, SLOTS * P], BF16, name="rounded")
             nc.scalar.copy(
                 rounded[:].rearrange("j (u p e) -> j u p e", u=2, e=2),
                 summed[:].rearrange("j (u e) p -> j u p e", e=2),
@@ -212,17 +225,16 @@ def tile_picked_twkflowbtop2twicp_none_po_kernel(
 
         def z2_first(i):
             c0, n = Z2_PIECES[i]
-            w = {name: new("%s%d" % (name, i), [P, SLOTS, n], F32, AFTER.get((name, i))) for name in ("b1", "gap12", "span", "top12", "gap3", "low")}
+            w = {name: new("%s%d" % (name, i), [P, SLOTS, n], F32, AFTER.get((name, i))) for name in ("gap12", "span", "top12", "gap3", "low")}
             work[i] = w
             for t in range(SLOTS):
-                nc.vector.tensor_copy(w["b1"][:, t, :], b_win[t][:].indirect(entries(l4, c0, n)))
-            for t in range(SLOTS):
-                nc.vector.tensor_tensor(w["gap12"][:, t, :], b_win[t][:].indirect(entries(l5, c0, n)), w["b1"][:, t, :], ALU.subtract)
+                nc.vector.tensor_tensor(w["gap12"][:, t, :], b_win[t][:].indirect(entries(l5, c0, n)), b1[:, t, c0 : c0 + n], ALU.subtract)
             nc.scalar.activation(flat(w["span"]), flat(w["gap12"]), ACT.Abs)
 
         def z2_top(i):
+            c0, n = Z2_PIECES[i]
             w = work[i]
-            nc.vector.scalar_tensor_tensor(flat(w["top12"]), flat(w["gap12"]), 0.0, flat(w["b1"]), ALU.max, ALU.add)
+            nc.vector.scalar_tensor_tensor(w["top12"][:], w["gap12"][:], 0.0, b1[:, :, c0 : c0 + n], ALU.max, ALU.add)
 
         def z2_third(i):
             c0, n = Z2_PIECES[i]
@@ -238,12 +250,13 @@ def tile_picked_twkflowbtop2twicp_none_po_kernel(
             c0, n = Z2_PIECES[i]
             w = work[i]
             w["lift"] = new("lift%d" % i, [P, SLOTS, n], F32, AFTER.get(("lift", i)))
-            w["bf"] = new("z2_bf%d" % i, [P, SLOTS * n], BF16)
+            w["bf"] = new("z2_bf%d" % i, [P, SLOTS * n], BF16, AFTER.get(("bf", i)))
             if i < len(Z2_PIECES) - 1:
-                nc.scalar.activation(flat(w["lift"]), flat(w["low"]), ACT.Relu, scale=-3.0)
                 pairs = w["bf"][:].bitcast(F32).rearrange("p (v u) -> p v u", u=2)
                 for blk in range(n // P):
-                    turned = sum_round_turn((w["top12"], w["low"], w["lift"]), P * blk, (i, blk) == (0, 1))
+                    cols = slice(P * blk, P * (blk + 1))
+                    nc.scalar.activation(w["lift"][:, :, cols], w["low"][:, :, cols], ACT.Relu, scale=-3.0)
+                    turned = sum_round_turn((w["lift"], w["top12"], w["low"]), P * blk)
                     nc.scalar.copy(pairs[:, P * blk : P * (blk + 1), :], turned[:].rearrange("p u v -> p v u"))
             else:
                 nc.vector.scalar_tensor_tensor(flat(w["lift"]), flat(w["low"]), -2.0, flat(w["low"]), ALU.mult, ALU.max)
@@ -282,20 +295,12 @@ def tile_picked_twkflowbtop2twicp_none_po_kernel(
         z2_first(1)
         z2_top(1)
         z2_third(1)
-        z2_low(1)
         z2_quantise(0)
-        z2_sum(1)
         for t in range(SLOTS):
             scores(0, t)
-        z2_first(2)
-        z2_top(2)
-        z2_third(2)
-        z2_low(2)
+        z2_low(1)
+        z2_sum(1)
         z2_quantise(1)
-        for t in range(SLOTS):
-            scores(1, t)
-        z2_sum(2)
-        z2_quantise(2)
 
         out_rows = out_0.rearrange("(p t) c -> p t c", t=SLOTS)
         gate = new("gate", [P, SLOTS, V], F32)

@@ -20,9 +20,9 @@ ACT = mybir.ActivationFunctionType
 P = 128
 SLOTS = 4
 HALF = 256
-X_FIRST = 512
+X_FIRST = 256
 Z2_PIECES = ((0, 256), (256, 256))
-AFTER = {("lift", 0): "pull2", ("gap12", 1): "z_bf", ("low", 1): "z2_bf0"}
+AFTER = {("lift", 0): "pull2", ("span", 1): "rounded_last", ("top12", 1): "gap30", ("bf", 1): "z2_bf0"}
 
 
 def tile_picked_twkflowbtop2twicp_none_po_kernel(
@@ -69,8 +69,8 @@ def tile_picked_twkflowbtop2twicp_none_po_kernel(
         ww_raw = [new("ww_raw%d" % i, [P, H // 2], I32) for i in range(3)]
         load_scale_rows(xs, x_scales)
         l_offs = load_list("l_offs", offs)
-        nc.sync.dma_start(xw[:, X_FIRST:T], x_rows[:, X_FIRST:T])
         l_two = load_list("l_two", two)
+        nc.sync.dma_start(xw[:, X_FIRST:T], x_rows[:, X_FIRST:T])
         l_three = load_list("l_three", three)
 
         nc.sync.dma_start(ww_raw[0][:], w1_words[0].bitcast(I32))
@@ -105,11 +105,11 @@ def tile_picked_twkflowbtop2twicp_none_po_kernel(
         def deal_weight(i):
             words = new("ww%d" % i, [P, 2 * H], U8)
             scales = new("ws%d" % i, [P, H], U8)
-            nc.vector.tensor_copy(
+            nc.gpsimd.tensor_copy(
                 words[:].bitcast(I32).rearrange("p (t b w) -> p t b w", t=SLOTS, w=4),
                 ww_raw[i][:].rearrange("p (b t w) -> p t b w", t=SLOTS, w=4),
             )
-            nc.vector.tensor_copy(
+            nc.gpsimd.tensor_copy(
                 scales[:].bitcast(I32).rearrange("p (t b w) -> p t b w", t=SLOTS, w=2),
                 ws_raw[i][:].bitcast(I32).rearrange("p (b t w) -> p t b w", t=SLOTS, w=2),
             )
@@ -129,30 +129,36 @@ def tile_picked_twkflowbtop2twicp_none_po_kernel(
             return bank
 
         s_offs = pick_scales("s_offs", l_offs)
+        s_two = pick_scales("s_two", l_two)
         x_offs = (pick_words("x_offs", l_offs), s_offs)
         w1 = deal_weight(0)
-        x_two = (pick_words("x_two", l_two, "ws_raw0"), pick_scales("s_two", l_two))
+        x_two = (pick_words("x_two", l_two), s_two)
         w2 = deal_weight(1)
 
         gain_bank = psum.tile([P, SLOTS, P], F32, name="summed", tag="summed")
         for t in range(SLOTS):
             nc.tensor.transpose(gain_bank[:, t, :], gain_rows[:, P * t : P * (t + 1)], ident[:])
+        gain_cols = new("gain_cols", [P, SLOTS, 2], F32)
+        nc.scalar.copy(gain_cols[:], gain_bank[:, :, 0:2])
         half_sign = new("half_sign", [P, SLOTS, 1], F32)
-        nc.vector.tensor_scalar(half_sign[:], gain_bank[:, :, 1:2], 0.0, 0.5, ALU.is_ge, ALU.subtract)
+        nc.gpsimd.tensor_scalar(half_sign[:], gain_cols[:, :, 1:2], 0.0, 0.5, ALU.is_ge, ALU.subtract)
         gains = new("gains", [P, SLOTS, 2], F32)
-        nc.vector.tensor_tensor(gains[:], gain_bank[:, :, 0:2], half_sign[:].to_broadcast([P, SLOTS, 2]), ALU.mult)
+        nc.gpsimd.tensor_tensor(gains[:], gain_cols[:], half_sign[:].to_broadcast([P, SLOTS, 2]), ALU.mult)
 
-        x_three = (pick_words("x_three", l_three, "ws_raw1"), pick_scales("s_three", l_three, "ww_raw1"))
+        x_three = (pick_words("x_three", l_three), pick_scales("s_three", l_three))
         w3 = deal_weight(2)
 
         y_win = [new("y_win%d" % t, [P, 2 * S], F32) for t in range(SLOTS)]
         d_win = [new("d_win%d" % t, [P, 2 * S], F32) for t in range(SLOTS)]
         b_win = [new("b_win%d" % t, [P, 2 * V], F32) for t in range(SLOTS)]
         for pair in range(2):
-            for t in (2 * pair, 2 * pair + 1):
-                bank = project(w1, x_offs, t)
-                nc.scalar.copy(y_win[t][:, 0:S], bank[:])
-                nc.scalar.copy(y_win[t ^ 1][:, S : 2 * S], bank[:])
+            first, second = 2 * pair, 2 * pair + 1
+            bank = project(w1, x_offs, first)
+            nc.scalar.copy(y_win[first][:, 0:S], bank[:])
+            nc.scalar.copy(y_win[second][:, S : 2 * S], bank[:])
+            bank = project(w1, x_offs, second)
+            nc.scalar.copy(y_win[first][:, S : 2 * S], bank[:])
+            nc.scalar.copy(y_win[second][:, 0:S], bank[:])
             for t in (2 * pair, 2 * pair + 1):
                 bank = project(w2, x_two, t)
                 nc.scalar.activation(d_win[t][:, 0:S], bank[:], ACT.Copy, scale=gains[:, t, 0:1])
@@ -181,14 +187,12 @@ def tile_picked_twkflowbtop2twicp_none_po_kernel(
         z_term2(SLOTS - 1)
         term1 = new("term1", [P, SLOTS, S], F32, "pull2")
         b1 = new("b1", [P, SLOTS, V], F32, "y_win3")
-        for h in range(2):
-            cols = slice(HALF * h, HALF * (h + 1))
-            for t in range(SLOTS):
-                nc.gpsimd.tensor_tensor(term1[:, t, cols], b_win[t][:, V + HALF * h : V + HALF * (h + 1)], d_win[t][:, S + HALF * h : S + HALF * (h + 1)], ALU.mult)
+        for t in range(SLOTS):
+            nc.gpsimd.tensor_tensor(term1[:, t, :], b_win[t][:, V : 2 * V], d_win[t][:, S : 2 * S], ALU.mult)
         for t in range(SLOTS):
             nc.vector.tensor_copy(b1[:, t, :], b_win[t][:].indirect(l4[:]))
 
-        def sum_round_turn(terms, c0):
+        def sum_round_turn(terms, c0, last=False):
             summed = psum.tile([P, SLOTS, P], F32, name="summed", tag="summed")
             for t in range(SLOTS):
                 for i, term in enumerate(terms):
@@ -196,7 +200,7 @@ def tile_picked_twkflowbtop2twicp_none_po_kernel(
                         summed[:, t, :], term[:, t, c0 : c0 + P], ident[:],
                         start=(i == 0), stop=(i == len(terms) - 1), is_transpose=True,
                     )
-            rounded = ring.tile([P, SLOTS * P], BF16, name="rounded")
+            rounded = new("rounded_last", [P, SLOTS * P], BF16) if last else ring.tile([P, SLOTS * P], BF16, name="rounded")
             nc.scalar.copy(
                 rounded[:].rearrange("j (u p e) -> j u p e", u=2, e=2),
                 summed[:].rearrange("j (u e) p -> j u p e", e=2),
@@ -209,7 +213,7 @@ def tile_picked_twkflowbtop2twicp_none_po_kernel(
         z_bf = new("z_bf", [P, SLOTS * S], BF16)
         z_pairs = z_bf[:].bitcast(F32).rearrange("p (t m u) -> p t m u", t=SLOTS, u=2)
         for blk in range(S // P):
-            turned = sum_round_turn((term1, term2), P * blk)
+            turned = sum_round_turn((term1, term2), P * blk, blk == S // P - 1)
             nc.scalar.copy(z_pairs[:, :, 32 * blk : 32 * (blk + 1), :], turned[:].rearrange("p u (m t) -> p t m u", t=SLOTS))
         z_codes = new("z_codes", [P, S], U32)
         z_scales = new("z_scales", [P, S], U8)
@@ -218,6 +222,8 @@ def tile_picked_twkflowbtop2twicp_none_po_kernel(
         z2_scales = new("z2_scales", [P, V], U8)
         s_bank = [psum.tile([P, V], F32, name="product", tag="product", bufs=4) for t in range(SLOTS)]
         s_win = [new("s_win%d" % t, [P, V], F32) for t in range(SLOTS)]
+        gate_win = new("gate_win", [P, 2 * V], F32)
+        nc.vector.memset(gate_win[:, V : 2 * V], 0.0)
         work = {}
 
         def flat(tile):
@@ -284,6 +290,8 @@ def tile_picked_twkflowbtop2twicp_none_po_kernel(
                 start=True,
                 stop=True,
             )
+            if t == 0:
+                nc.scalar.activation(gate_win[:, cols], s_bank[t][:, cols], ACT.Sigmoid, scale=0.0625)
             nc.scalar.activation(s_win[t][:, cols], s_bank[t][:, cols], ACT.Copy, scale=0.0625)
 
         z2_first(0)
@@ -295,10 +303,10 @@ def tile_picked_twkflowbtop2twicp_none_po_kernel(
         z2_first(1)
         z2_top(1)
         z2_third(1)
+        z2_low(1)
         z2_quantise(0)
         for t in range(SLOTS):
             scores(0, t)
-        z2_low(1)
         z2_sum(1)
         z2_quantise(1)
 
@@ -314,6 +322,9 @@ def tile_picked_twkflowbtop2twicp_none_po_kernel(
 
         def gated(t):
             scores(len(Z2_PIECES) - 1, t)
+            if t == 0:
+                nc.vector.tensor_tensor(st_win[t][:], gate_win[:].indirect(l7[:]), s_win[t][:], ALU.mult)
+                return
             for h in range(2):
                 nc.scalar.activation(gate[:, t, HALF * h : HALF * (h + 1)], s_win[t][:].indirect(entries(l7, HALF * h, HALF)), ACT.Sigmoid)
             nc.vector.tensor_tensor(st_win[t][:], s_win[t][:], gate[:, t, :], ALU.mult)

@@ -22,7 +22,7 @@ SLOTS = 4
 HALF = 256
 X_FIRST = 256
 Z2_PIECES = ((0, 256), (256, 256))
-AFTER = {("lift", 0): "pull2", ("span", 1): "rounded_last", ("top12", 1): "gap30", ("bf", 1): "z2_bf0"}
+AFTER = {("lift", 0): "pull2", ("gap12", 1): "gap120", ("span", 1): "rounded_last", ("top12", 1): "gap30", ("bf", 1): "z2_bf0"}
 
 
 def tile_picked_twkflowbtop2twicp_none_po_kernel(
@@ -61,8 +61,8 @@ def tile_picked_twkflowbtop2twicp_none_po_kernel(
         ident = new("ident", [P, P], F32)
         make_identity(nc, ident[:])
 
-        warm = new("warm", [P, 1], F32)
-        nc.scalar.activation(warm[:], ident[:, 0:1], ACT.Sigmoid)
+        gate_win = new("gate_win", [P, 2 * V], F32)
+        nc.scalar.activation(gate_win[:, V : 2 * V], ident[:, 0:1].to_broadcast([P, V]), ACT.Sigmoid)
         xw = new("xw", [P, T], I32)
         x_rows = x_words[0].rearrange("p n t -> p (n t)").bitcast(I32)
         nc.sync.dma_start(xw[:, 0:X_FIRST], x_rows[:, 0:X_FIRST])
@@ -71,10 +71,10 @@ def tile_picked_twkflowbtop2twicp_none_po_kernel(
         l_offs = load_list("l_offs", offs)
         l_two = load_list("l_two", two)
         nc.sync.dma_start(xw[:, X_FIRST:T], x_rows[:, X_FIRST:T])
-        l_three = load_list("l_three", three)
 
-        nc.sync.dma_start(ww_raw[0][:], w1_words[0].bitcast(I32))
         load_scale_rows(ws_raw[0], w1_scales)
+        nc.sync.dma_start(ww_raw[0][:], w1_words[0].bitcast(I32))
+        l_three = load_list("l_three", three)
         l1 = load_list("l1", n1)
         l2 = load_list("l2", n2)
         nc.sync.dma_start(ww_raw[1][:], w2_words[0].bitcast(I32))
@@ -102,14 +102,14 @@ def tile_picked_twkflowbtop2twicp_none_po_kernel(
             nc.vector.tensor_copy(picked[:], xw[:].bitcast(U32).indirect(lst[:]))
             return picked
 
-        def deal_weight(i):
-            words = new("ww%d" % i, [P, 2 * H], U8)
-            scales = new("ws%d" % i, [P, H], U8)
-            nc.gpsimd.tensor_copy(
+        def deal_weight(i, words_tag=None, scales_tag=None):
+            words = new("ww%d" % i, [P, 2 * H], U8, words_tag)
+            scales = new("ws%d" % i, [P, H], U8, scales_tag)
+            nc.vector.tensor_copy(
                 words[:].bitcast(I32).rearrange("p (t b w) -> p t b w", t=SLOTS, w=4),
                 ww_raw[i][:].rearrange("p (b t w) -> p t b w", t=SLOTS, w=4),
             )
-            nc.gpsimd.tensor_copy(
+            nc.vector.tensor_copy(
                 scales[:].bitcast(I32).rearrange("p (t b w) -> p t b w", t=SLOTS, w=2),
                 ws_raw[i][:].bitcast(I32).rearrange("p (b t w) -> p t b w", t=SLOTS, w=2),
             )
@@ -131,43 +131,21 @@ def tile_picked_twkflowbtop2twicp_none_po_kernel(
         s_offs = pick_scales("s_offs", l_offs)
         s_two = pick_scales("s_two", l_two)
         x_offs = (pick_words("x_offs", l_offs), s_offs)
-        w1 = deal_weight(0)
         x_two = (pick_words("x_two", l_two), s_two)
-        w2 = deal_weight(1)
-
-        gain_bank = psum.tile([P, SLOTS, P], F32, name="summed", tag="summed")
-        for t in range(SLOTS):
-            nc.tensor.transpose(gain_bank[:, t, :], gain_rows[:, P * t : P * (t + 1)], ident[:])
-        gain_cols = new("gain_cols", [P, SLOTS, 2], F32)
-        nc.scalar.copy(gain_cols[:], gain_bank[:, :, 0:2])
-        half_sign = new("half_sign", [P, SLOTS, 1], F32)
-        nc.gpsimd.tensor_scalar(half_sign[:], gain_cols[:, :, 1:2], 0.0, 0.5, ALU.is_ge, ALU.subtract)
-        gains = new("gains", [P, SLOTS, 2], F32)
-        nc.gpsimd.tensor_tensor(gains[:], gain_cols[:], half_sign[:].to_broadcast([P, SLOTS, 2]), ALU.mult)
-
+        w1 = deal_weight(0)
         x_three = (pick_words("x_three", l_three), pick_scales("s_three", l_three))
-        w3 = deal_weight(2)
 
         y_win = [new("y_win%d" % t, [P, 2 * S], F32) for t in range(SLOTS)]
         d_win = [new("d_win%d" % t, [P, 2 * S], F32) for t in range(SLOTS)]
         b_win = [new("b_win%d" % t, [P, 2 * V], F32) for t in range(SLOTS)]
-        for pair in range(2):
-            first, second = 2 * pair, 2 * pair + 1
+        for first in (0, 2):
+            second = first + 1
             bank = project(w1, x_offs, first)
             nc.scalar.copy(y_win[first][:, 0:S], bank[:])
             nc.scalar.copy(y_win[second][:, S : 2 * S], bank[:])
             bank = project(w1, x_offs, second)
             nc.scalar.copy(y_win[first][:, S : 2 * S], bank[:])
             nc.scalar.copy(y_win[second][:, 0:S], bank[:])
-            for t in (2 * pair, 2 * pair + 1):
-                bank = project(w2, x_two, t)
-                nc.scalar.activation(d_win[t][:, 0:S], bank[:], ACT.Copy, scale=gains[:, t, 0:1])
-        for t in range(SLOTS):
-            bank = project(w3, x_three, t)
-            nc.scalar.activation(b_win[t][:, 0:V], bank[:], ACT.Copy, scale=gains[:, t, 1:2])
-
-        for t in range(SLOTS):
-            nc.scalar.activation(b_win[t][:, V : 2 * V], d_win[t][:, 0:S], ACT.Copy, scale=2.0)
 
         pull2 = new("pull2", [P, SLOTS, S], F32)
         term2 = new("term2", [P, SLOTS, S], F32)
@@ -181,10 +159,28 @@ def tile_picked_twkflowbtop2twicp_none_po_kernel(
             nc.vector.tensor_tensor(term2[:, t, :], d_win[t][:].indirect(l3[:]), pull2[:, t, :], ALU.mult)
 
         z_pulls(0)
-        for t in range(1, SLOTS):
-            z_pulls(t)
-            z_term2(t - 1)
-        z_term2(SLOTS - 1)
+        z_pulls(1)
+        w2 = deal_weight(1, "y_win0", "y_win1")
+        w3 = deal_weight(2, "ww_raw1", "ws_raw1")
+        gain_bank = psum.tile([P, SLOTS, P], F32, name="summed", tag="summed")
+        for t in range(SLOTS):
+            nc.tensor.transpose(gain_bank[:, t, :], gain_rows[:, P * t : P * (t + 1)], ident[:])
+        half_sign = new("half_sign", [P, SLOTS, 1], F32, "ww_raw2")
+        nc.vector.tensor_scalar(half_sign[:], gain_bank[:, :, 1:2], 0.0, 0.5, ALU.is_ge, ALU.subtract)
+        gains = new("gains", [P, SLOTS, 2], F32)
+        nc.vector.tensor_tensor(gains[:], gain_bank[:, :, 0:2], half_sign[:].to_broadcast([P, SLOTS, 2]), ALU.mult)
+        for t in range(SLOTS):
+            bank = project(w2, x_two, t)
+            nc.scalar.activation(d_win[t][:, 0:S], bank[:], ACT.Copy, scale=gains[:, t, 0:1])
+        for t in range(SLOTS):
+            bank = project(w3, x_three, t)
+            nc.scalar.activation(b_win[t][:, 0:V], bank[:], ACT.Copy, scale=gains[:, t, 1:2])
+        for t in range(SLOTS):
+            nc.scalar.activation(b_win[t][:, V : 2 * V], d_win[t][:, 0:S], ACT.Copy, scale=2.0)
+        z_pulls(2)
+        z_pulls(3)
+        for t in range(SLOTS):
+            z_term2(t)
         term1 = new("term1", [P, SLOTS, S], F32, "pull2")
         b1 = new("b1", [P, SLOTS, V], F32, "y_win3")
         for t in range(SLOTS):
@@ -222,8 +218,6 @@ def tile_picked_twkflowbtop2twicp_none_po_kernel(
         z2_scales = new("z2_scales", [P, V], U8)
         s_bank = [psum.tile([P, V], F32, name="product", tag="product", bufs=4) for t in range(SLOTS)]
         s_win = [new("s_win%d" % t, [P, V], F32) for t in range(SLOTS)]
-        gate_win = new("gate_win", [P, 2 * V], F32)
-        nc.vector.memset(gate_win[:, V : 2 * V], 0.0)
         work = {}
 
         def flat(tile):

from contextlib import ExitStack

import concourse.mybir as mybir
from concourse.masks import make_identity

K, T, S, V, H = 512, 2048, 512, 512, 512
FLOPS = 4 * 2 * 512 * 512 * 512

F32 = mybir.dt.float32
BF16 = mybir.dt.bfloat16
I32 = mybir.dt.int32
U32 = mybir.dt.uint32
U16 = mybir.dt.uint16
U8 = mybir.dt.uint8
FP8X4 = mybir.dt.float8_e4m3fn_x4
FP4X4 = mybir.dt.float4_e2m1fn_x4
ALU = mybir.AluOpType
ACT = mybir.ActivationFunctionType

P = 128
SLOTS = 4
HALF = 256
X_FIRST = 256
Z2_PIECES = ((0, 256), (256, 256))
AFTER = {("lift", 0): "pull2", ("gap12", 1): "gap120", ("span", 1): "rounded_last", ("top12", 1): "gap30", ("bf", 1): "z2_bf0"}


def tile_picked_twkflowbtop2twicp_none_po_kernel(
    tc, x_words, x_scales, w1_words, w1_scales, w2_words, w2_scales, w3_words, w3_scales,
    ga, gb, offs, two, n1, n2, n3, three, n4, n5, n6, n7, out_0, out_1, out_2,
):
    nc = tc.nc
    with ExitStack() as ctx:
        keep = ctx.enter_context(tc.tile_pool(name="keep", bufs=1))
        ring = ctx.enter_context(tc.tile_pool(name="ring", bufs=2))
        psum = ctx.enter_context(tc.psum_pool(name="psum", bufs=2))

        def new(name, shape, dtype, tag=None):
            return keep.tile(shape, dtype, name=name, tag=tag or name, align_bytes=64)

        def load_list(name, src):
            lst = new(name, [P, 32], U16)
            nc.sync.dma_start(lst[:], src)
            return lst

        def entries(lst, c0, n):
            return lst[:, c0 // 16 : (c0 + n) // 16]

        def load_scale_rows(plane, src):
            rows = src[0].bitcast(I32)
            for q in range(4):
                nc.sync.dma_start(plane[32 * q : 32 * q + 4, :].bitcast(I32), rows[4 * q : 4 * q + 4, :])

        xs = new("xs", [P, T], U8)
        nc.gpsimd.memset(xs[:].bitcast(I32), 0)
        ws_raw = [new("ws_raw%d" % i, [P, H], U8) for i in range(3)]
        for plane in ws_raw:
            nc.vector.memset(plane[:].bitcast(I32), 0)
        gain_rows = new("gain_rows", [P, H], F32)
        nc.gpsimd.memset(gain_rows[:], 0.0)
        ident = new("ident", [P, P], F32)
        make_identity(nc, ident[:])

        gate_win = new("gate_win", [P, 2 * V], F32)
        nc.scalar.activation(gate_win[:, V : 2 * V], ident[:, 0:1].to_broadcast([P, V]), ACT.Sigmoid)
        xw = new("xw", [P, T], I32)
        x_rows = x_words[0].rearrange("p n t -> p (n t)").bitcast(I32)
        nc.sync.dma_start(xw[:, 0:X_FIRST], x_rows[:, 0:X_FIRST])
        ww_raw = [new("ww_raw%d" % i, [P, H // 2], I32) for i in range(3)]
        load_scale_rows(xs, x_scales)
        l_offs = load_list("l_offs", offs)
        l_two = load_list("l_two", two)
        nc.sync.dma_start(xw[:, X_FIRST:T], x_rows[:, X_FIRST:T])

        load_scale_rows(ws_raw[0], w1_scales)
        nc.sync.dma_start(ww_raw[0][:], w1_words[0].bitcast(I32))
        l_three = load_list("l_three", three)
        l1 = load_list("l1", n1)
        l2 = load_list("l2", n2)
        nc.sync.dma_start(ww_raw[1][:], w2_words[0].bitcast(I32))
        load_scale_rows(ws_raw[1], w2_scales)
        for row, gain in enumerate((ga, gb)):
            nc.sync.dma_start(
                gain_rows[row : row + 1, :].rearrange("o (t b c) -> o t b c", t=SLOTS, c=8),
                gain.rearrange("(b t c) o -> o t b c", t=SLOTS, c=8),
            )
        l3 = load_list("l3", n3)
        nc.sync.dma_start(ww_raw[2][:], w3_words[0].bitcast(I32))
        load_scale_rows(ws_raw[2], w3_scales)
        l4 = load_list("l4", n4)
        l5 = load_list("l5", n5)
        l6 = load_list("l6", n6)
        l7 = load_list("l7", n7)

        def pick_scales(name, lst, tag=None):
            picked = new(name, [P, S], U8, tag)
            nc.vector.tensor_copy(picked[:], xs[:].indirect(lst[:]))
            return picked

        def pick_words(name, lst, tag=None):
            picked = new(name, [P, S], U32, tag)
            nc.vector.tensor_copy(picked[:], xw[:].bitcast(U32).indirect(lst[:]))
            return picked

        def deal_weight(i, words_tag=None, scales_tag=None):
            words = new("ww%d" % i, [P, 2 * H], U8, words_tag)
            scales = new("ws%d" % i, [P, H], U8, scales_tag)
            nc.vector.tensor_copy(
                words[:].bitcast(I32).rearrange("p (t b w) -> p t b w", t=SLOTS, w=4),
                ww_raw[i][:].rearrange("p (b t w) -> p t b w", t=SLOTS, w=4),
            )
            nc.vector.tensor_copy(
                scales[:].bitcast(I32).rearrange("p (t b w) -> p t b w", t=SLOTS, w=2),
                ws_raw[i][:].bitcast(I32).rearrange("p (b t w) -> p t b w", t=SLOTS, w=2),
            )
            return words, scales

        def project(weight, picked, t):
            bank = psum.tile([P, S], F32, name="product", tag="product", bufs=4)
            nc.tensor.matmul_mx(
                bank[:],
                lhsT=weight[0][:, 2 * P * t : 2 * P * (t + 1)].bitcast(FP4X4),
                lhsT_scale=weight[1][:, P * t : P * (t + 1)],
                rhs=picked[0][:].bitcast(FP8X4),
                rhs_scale=picked[1][:],
                start=True,
                stop=True,
            )
            return bank

        s_offs = pick_scales("s_offs", l_offs)
        s_two = pick_scales("s_two", l_two)
        x_offs = (pick_words("x_offs", l_offs), s_offs)
        x_two = (pick_words("x_two", l_two), s_two)
        w1 = deal_weight(0)
        x_three = (pick_words("x_three", l_three), pick_scales("s_three", l_three))

        y_win = [new("y_win%d" % t, [P, 2 * S], F32) for t in range(SLOTS)]
        d_win = [new("d_win%d" % t, [P, 2 * S], F32) for t in range(SLOTS)]
        b_win = [new("b_win%d" % t, [P, 2 * V], F32) for t in range(SLOTS)]
        for first in (0, 2):
            second = first + 1
            bank = project(w1, x_offs, first)
            nc.scalar.copy(y_win[first][:, 0:S], bank[:])
            nc.scalar.copy(y_win[second][:, S : 2 * S], bank[:])
            bank = project(w1, x_offs, second)
            nc.scalar.copy(y_win[first][:, S : 2 * S], bank[:])
            nc.scalar.copy(y_win[second][:, 0:S], bank[:])

        pull2 = new("pull2", [P, SLOTS, S], F32)
        term2 = new("term2", [P, SLOTS, S], F32)

        def z_pulls(t):
            y_plain = y_win[t ^ 1][:, S : 2 * S]
            nc.vector.tensor_tensor(d_win[t][:, S : 2 * S], y_win[t][:].indirect(l1[:]), y_plain, ALU.subtract)
            nc.vector.tensor_tensor(pull2[:, t, :], y_win[t][:].indirect(l2[:]), y_plain, ALU.subtract)

        def z_term2(t):
            nc.vector.tensor_tensor(term2[:, t, :], d_win[t][:].indirect(l3[:]), pull2[:, t, :], ALU.mult)

        z_pulls(0)
        z_pulls(1)
        w2 = deal_weight(1, "y_win0", "y_win1")
        w3 = deal_weight(2, "ww_raw1", "ws_raw1")
        gain_bank = psum.tile([P, SLOTS, P], F32, name="summed", tag="summed")
        for t in range(SLOTS):
            nc.tensor.transpose(gain_bank[:, t, :], gain_rows[:, P * t : P * (t + 1)], ident[:])
        half_sign = new("half_sign", [P, SLOTS, 1], F32, "ww_raw2")
        nc.vector.tensor_scalar(half_sign[:], gain_bank[:, :, 1:2], 0.0, 0.5, ALU.is_ge, ALU.subtract)
        gains = new("gains", [P, SLOTS, 2], F32)
        nc.vector.tensor_tensor(gains[:], gain_bank[:, :, 0:2], half_sign[:].to_broadcast([P, SLOTS, 2]), ALU.mult)
        for t in range(SLOTS):
            bank = project(w2, x_two, t)
            nc.scalar.activation(d_win[t][:, 0:S], bank[:], ACT.Copy, scale=gains[:, t, 0:1])
        for t in range(SLOTS):
            bank = project(w3, x_three, t)
            nc.scalar.activation(b_win[t][:, 0:V], bank[:], ACT.Copy, scale=gains[:, t, 1:2])
        for t in range(SLOTS):
            nc.scalar.activation(b_win[t][:, V : 2 * V], d_win[t][:, 0:S], ACT.Copy, scale=2.0)
        z_pulls(2)
        z_pulls(3)
        for t in range(SLOTS):
            z_term2(t)
        term1 = new("term1", [P, SLOTS, S], F32, "pull2")
        b1 = new("b1", [P, SLOTS, V], F32, "y_win3")
        for t in range(SLOTS):
            nc.gpsimd.tensor_tensor(term1[:, t, :], b_win[t][:, V : 2 * V], d_win[t][:, S : 2 * S], ALU.mult)
        for t in range(SLOTS):
            nc.vector.tensor_copy(b1[:, t, :], b_win[t][:].indirect(l4[:]))

        def sum_round_turn(terms, c0, last=False):
            summed = psum.tile([P, SLOTS, P], F32, name="summed", tag="summed")
            for t in range(SLOTS):
                for i, term in enumerate(terms):
                    nc.tensor.matmul(
                        summed[:, t, :], term[:, t, c0 : c0 + P], ident[:],
                        start=(i == 0), stop=(i == len(terms) - 1), is_transpose=True,
                    )
            rounded = new("rounded_last", [P, SLOTS * P], BF16) if last else ring.tile([P, SLOTS * P], BF16, name="rounded")
            nc.scalar.copy(
                rounded[:].rearrange("j (u p e) -> j u p e", u=2, e=2),
                summed[:].rearrange("j (u e) p -> j u p e", e=2),
            )
            turned = psum.tile([P, 2, P], F32, name="turned", tag="turned")
            for u in range(2):
                nc.tensor.transpose(turned[:, u, :], rounded[:].bitcast(F32)[:, P * u : P * (u + 1)], ident[:])
            return turned

        z_bf = new("z_bf", [P, SLOTS * S], BF16)
        z_pairs = z_bf[:].bitcast(F32).rearrange("p (t m u) -> p t m u", t=SLOTS, u=2)
        for blk in range(S // P):
            turned = sum_round_turn((term1, term2), P * blk, blk == S // P - 1)
            nc.scalar.copy(z_pairs[:, :, 32 * blk : 32 * (blk + 1), :], turned[:].rearrange("p u (m t) -> p t m u", t=SLOTS))
        z_codes = new("z_codes", [P, S], U32)
        z_scales = new("z_scales", [P, S], U8)

        z2_codes = new("z2_codes", [P, V], U32)
        z2_scales = new("z2_scales", [P, V], U8)
        s_bank = [psum.tile([P, V], F32, name="product", tag="product", bufs=4) for t in range(SLOTS)]
        s_win = [new("s_win%d" % t, [P, V], F32) for t in range(SLOTS)]
        work = {}

        def flat(tile):
            return tile[:].rearrange("p t c -> p (t c)")

        def z2_first(i):
            c0, n = Z2_PIECES[i]
            w = {name: new("%s%d" % (name, i), [P, SLOTS, n], F32, AFTER.get((name, i))) for name in ("gap12", "span", "top12", "gap3", "low")}
            work[i] = w
            for t in range(SLOTS):
                nc.vector.tensor_tensor(w["gap12"][:, t, :], b_win[t][:].indirect(entries(l5, c0, n)), b1[:, t, c0 : c0 + n], ALU.subtract)
            nc.scalar.activation(flat(w["span"]), flat(w["gap12"]), ACT.Abs)

        def z2_top(i):
            c0, n = Z2_PIECES[i]
            w = work[i]
            nc.vector.scalar_tensor_tensor(w["top12"][:], w["gap12"][:], 0.0, b1[:, :, c0 : c0 + n], ALU.max, ALU.add)

        def z2_third(i):
            c0, n = Z2_PIECES[i]
            w = work[i]
            for t in range(SLOTS):
                nc.vector.tensor_tensor(w["gap3"][:, t, :], b_win[t][:].indirect(entries(l6, c0, n)), w["top12"][:, t, :], ALU.subtract)

        def z2_low(i):
            w = work[i]
            nc.vector.scalar_tensor_tensor(flat(w["low"]), flat(w["gap3"]), -1.0, flat(w["span"]), ALU.mult, ALU.min)

        def z2_sum(i):
            c0, n = Z2_PIECES[i]
            w = work[i]
            w["lift"] = new("lift%d" % i, [P, SLOTS, n], F32, AFTER.get(("lift", i)))
            w["bf"] = new("z2_bf%d" % i, [P, SLOTS * n], BF16, AFTER.get(("bf", i)))
            if i < len(Z2_PIECES) - 1:
                pairs = w["bf"][:].bitcast(F32).rearrange("p (v u) -> p v u", u=2)
                for blk in range(n // P):
                    cols = slice(P * blk, P * (blk + 1))
                    nc.scalar.activation(w["lift"][:, :, cols], w["low"][:, :, cols], ACT.Relu, scale=-3.0)
                    turned = sum_round_turn((w["lift"], w["top12"], w["low"]), P * blk)
                    nc.scalar.copy(pairs[:, P * blk : P * (blk + 1), :], turned[:].rearrange("p u v -> p v u"))
            else:
                nc.vector.scalar_tensor_tensor(flat(w["lift"]), flat(w["low"]), -2.0, flat(w["low"]), ALU.mult, ALU.max)
                nc.vector.tensor_tensor(
                    w["bf"][:].rearrange("p (c i t) -> p c t i", i=2, t=SLOTS),
                    w["lift"][:].rearrange("p t (c i) -> p c t i", i=2),
                    w["top12"][:].rearrange("p t (c i) -> p c t i", i=2),
                    ALU.add,
                )

        def z2_quantise(i):
            c0, n = Z2_PIECES[i]
            cols = slice(c0, c0 + n)
            nc.vector.quantize_mx(z2_codes[:, cols].bitcast(FP8X4), z2_scales[:, cols], work[i]["bf"][:])

        def scores(i, t):
            c0, n = Z2_PIECES[i]
            cols = slice(c0, c0 + n)
            nc.tensor.matmul_mx(
                s_bank[t][:, cols],
                lhsT=z_codes[:, P * t : P * (t + 1)].bitcast(FP8X4),
                lhsT_scale=z_scales[:, P * t : P * (t + 1)],
                rhs=z2_codes[:, cols].bitcast(FP8X4),
                rhs_scale=z2_scales[:, cols],
                start=True,
                stop=True,
            )
            if t == 0:
                nc.scalar.activation(gate_win[:, cols], s_bank[t][:, cols], ACT.Sigmoid, scale=0.0625)
            nc.scalar.activation(s_win[t][:, cols], s_bank[t][:, cols], ACT.Copy, scale=0.0625)

        z2_first(0)
        z2_top(0)
        z2_third(0)
        z2_low(0)
        z2_sum(0)
        nc.vector.quantize_mx(z_codes[:].bitcast(FP8X4), z_scales[:], z_bf[:])
        z2_first(1)
        z2_top(1)
        z2_third(1)
        z2_low(1)
        z2_quantise(0)
        for t in range(SLOTS):
            scores(0, t)
        z2_sum(1)
        z2_quantise(1)

        out_rows = out_0.rearrange("(p t) c -> p t c", t=SLOTS)
        gate = new("gate", [P, SLOTS, V], F32)
        st_win = [new("st_win%d" % t, [P, V], F32) for t in range(SLOTS)]
        other = [new("other%d" % h, [P, SLOTS, HALF], F32) for h in range(2)]
        res = [new("res%d" % h, [P, SLOTS, HALF], F32) for h in range(2)]
        res_bf = [new("res_bf%d" % h, [P, SLOTS * HALF], BF16) for h in range(2)]
        res_codes = new("res_codes", [P, V], U32)
        res_scales = new("res_scales", [P, V], U8)
        out_words = out_1[0].rearrange("p c t -> p (c t)").bitcast(I32)

        def gated(t):
            scores(len(Z2_PIECES) - 1, t)
            if t == 0:
                nc.vector.tensor_tensor(st_win[t][:], gate_win[:].indirect(l7[:]), s_win[t][:], ALU.mult)
                return
            for h in range(2):
                nc.scalar.activation(gate[:, t, HALF * h : HALF * (h + 1)], s_win[t][:].indirect(entries(l7, HALF * h, HALF)), ACT.Sigmoid)
            nc.vector.tensor_tensor(st_win[t][:], s_win[t][:], gate[:, t, :], ALU.mult)

        def fetch(t, h):
            nc.vector.tensor_copy(other[h][:, t, :], st_win[t][:].indirect(entries(l7, HALF * h, HALF)))

        def larger(t, h):
            cols = slice(HALF * h, HALF * (h + 1))
            nc.vector.tensor_tensor(res[h][:, t, :], st_win[t][:, cols], other[h][:, t, :], ALU.max)
            nc.sync.dma_start(out_rows[:, t, cols], res[h][:, t, :])

        def weave(engine_copy, h, c0, c1):
            engine_copy(
                res_bf[h][:, SLOTS * c0 : SLOTS * c1].rearrange("p (c i t) -> p c t i", i=4, t=SLOTS),
                res[h][:, :, c0:c1].rearrange("p t (c i) -> p c t i", i=4),
            )

        def hand_on(h):
            cols = slice(HALF * h, HALF * (h + 1))
            nc.vector.quantize_mx(res_codes[:, cols].bitcast(FP8X4), res_scales[:, cols], res_bf[h][:])
            nc.scalar.dma_start(out_words[:, cols], res_codes[:, cols].bitcast(I32))

        gated(0)
        fetch(0, 0)
        for t in range(1, SLOTS):
            gated(t)
            larger(t - 1, 0)
            fetch(t, 0)
        fetch(0, 1)
        larger(SLOTS - 1, 0)
        weave(nc.scalar.copy, 0, 0, HALF)
        for t in range(1, SLOTS):
            fetch(t, 1)
            larger(t - 1, 1)
        hand_on(0)
        larger(SLOTS - 1, 1)
        weave(nc.vector.tensor_copy, 1, 0, 160)
        weave(nc.scalar.copy, 1, 160, HALF)
        hand_on(1)
        scale_rows = out_2[0].bitcast(I32)
        for q in range(4):
            queue = nc.sync if q % 2 == 0 else nc.scalar
            queue.dma_start(scale_rows[4 * q : 4 * q + 4, :], res_scales[32 * q : 32 * q + 4, :].bitcast(I32))
